import numpy as np
import ml_dtypes


def mxq(x, axis, fmt="e4m3"):
    dtype, down = {"e4m3": (ml_dtypes.float8_e4m3fn, 7), "e5m2": (ml_dtypes.float8_e5m2, 14)}[fmt]
    v = np.moveaxis(np.asarray(x, np.float32).astype(ml_dtypes.bfloat16).astype(np.float64), axis, -1)
    blocks = v.reshape(v.shape[:-1] + (-1, 32))
    amax = np.abs(blocks).max(-1, keepdims=True)
    byte = np.maximum(np.where(amax > 0, np.frexp(amax)[1] - 1 + 127, 0) - down, 1)
    scale = np.exp2(byte - 127.0)
    codes = (blocks / scale).astype(np.float32).astype(dtype).astype(np.float64)
    return np.moveaxis((codes * scale).reshape(v.shape), -1, axis)


WIDE = False


def mx_kscale(k):
    if not WIDE:
        return np.ones(k)
    levels = np.array([10, -10, 5, -5, 0])
    if k % 512:
        return np.exp2(np.random.permutation(np.resize(levels, k // 32))).repeat(32)
    a = np.empty((k // 512, 16))
    for p in range(k // 512):
        a[p, :8] = np.random.permutation(np.resize(levels, 8))
        for g in range(8):
            far = levels[np.abs(levels - a[p, g]) >= 10]
            a[p, g + 8] = far[np.random.randint(len(far))]
    return np.exp2(a.ravel()).repeat(32)


def f64(x):
    return np.asarray(x).astype(np.float64)


def striped(idx):
    return np.tile(idx.reshape(-1, 16).T, (8, 1)).astype(np.uint16)


def unstriped(offs):
    return offs[:16].T.reshape(-1).astype(np.int64)


def pack_weight(w):
    k, n = w.shape
    w = f64(np.asarray(w, np.float32).astype(ml_dtypes.bfloat16)).reshape(k // 32, 32, n)
    amax = np.abs(w).max(1)
    byte = np.clip(np.where(amax > 0, np.frexp(amax)[1] - 1 + 127 - 7, 1), 1, 254)
    scaled = (w * np.exp2(127.0 - byte)[:, None, :]).reshape(k, n).astype(np.float32)
    words = np.ascontiguousarray(scaled.reshape(k // 512, 128, 4, n).transpose(0, 1, 3, 2)).astype(ml_dtypes.float8_e4m3fn).view(np.uint8)
    return words, np.ascontiguousarray(byte.astype(np.uint8).reshape(k // 512, 16, n))


def unpack_weight(words, scales):
    g, p, n, _ = words.shape
    vals = np.ascontiguousarray(words).view(ml_dtypes.float8_e4m3fn).astype(np.float64) * np.repeat(np.exp2(scales.astype(np.float64) - 127.0), 8, axis=1)[..., None]
    return vals.transpose(0, 1, 3, 2).reshape(g * 512, n)


def gelu(v):
    return 0.5 * v * (1.0 + np.tanh(np.sqrt(2.0 / np.pi) * (v + 0.044715 * v**3)))


K, T, D, S, V, N = 1024, 1024, 4, 1024, 256, 256
P = 2 ** 7


def setup_inputs():
    n = np.random.standard_normal
    s = mx_kscale(K)[:, None]
    words, scales = pack_weight(n((K, N)) / np.sqrt(K) / s)
    return {
        "xT": (n((K, T)) * s / np.sqrt(D)).astype(ml_dtypes.bfloat16).astype(np.float32),
        "w_words": words,
        "w_scales": scales,
        "b": (0.3 * n((N, 1))).astype(np.float32),
        "gate": np.tile(np.random.uniform(0.5, 1.5, (D, 1, V)), (1, P, 1)).astype(ml_dtypes.bfloat16).astype(np.float32),
        "offs": striped(np.concatenate([np.random.permutation(T)[:V] for _ in range(D)])),
    }


def reference(xT, w_words, w_scales, b, gate, offs):
    w = unpack_weight(w_words, w_scales)
    idx = unstriped(offs)
    x = sum(f64(gate)[d, :1] * f64(xT)[:, idx[d * V:(d + 1) * V]] for d in range(D))
    return gelu((w.T @ mxq(x, 0, "e4m3")) + f64(b))

@@ -1,0 +1,179 @@
+from contextlib import ExitStack
+
+import concourse.mybir as mybir
+from concourse.masks import make_identity
+
+K, T, D, V, N = 1024, 1024, 4, 256, 256
+FLOPS = 2 * K * N * V
+
+F32 = mybir.dt.float32
+BF16 = mybir.dt.bfloat16
+U32 = mybir.dt.uint32
+I32 = mybir.dt.int32
+U16 = mybir.dt.uint16
+U8 = mybir.dt.uint8
+FP8X4 = mybir.dt.float8_e4m3fn_x4
+ACT = mybir.ActivationFunctionType
+ALU = mybir.AluOpType
+
+P = 128
+PASSES = K // 512
+VB = V // P
+MB = N // P
+LOADS = ((0,512,768,1024,),(0,512,1024,),(0,512,1024,),(0,512,1024,),)
+PLAN = (("cast",0,0,512,"v",),("cast",0,512,768,"v",),("cast",0,768,1024,"v",),("cast",1,0,512,"s",),("cast",1,512,1024,"g",),("cast",2,0,512,"g",),("cast",2,512,768,"g",),("front",0,((0,0,),(0,1,),),"s",),("front",0,((1,0,),(1,1,),),"s",),("back",0,((0,0,),(0,1,),),(),),("front",0,((2,0,),(2,1,),(3,0,),(3,1,),),"s",),("back",0,((1,0,),(1,1,),),(),),("front",1,((0,0,),(0,1,),(1,0,),(1,1,),),"s",),("back",0,((2,0,),(2,1,),(3,0,),(3,1,),),(),),("front",1,((2,0,),(2,1,),(3,0,),(3,1,),),"s",),("back",1,((0,0,),(0,1,),(1,0,),(1,1,),),(),),("cast",2,768,1024,"v",),("cast",3,0,512,"g",),("cast",3,512,1024,"g",),("front",2,((0,0,),(0,1,),(1,0,),(1,1,),),"s",),("back",1,((2,0,),(2,1,),(3,0,),(3,1,),),((3,0,),(3,1,),),),("front",2,((2,0,),(2,1,),(3,0,),(3,1,),),"s",),("back",2,((0,0,),(0,1,),(1,0,),(1,1,),),(),),("out",0,0,"v",),("out",0,1,"v",),("quant",0,(0,1,),),("front",3,((0,0,),(1,0,),),"s",),("back",2,((2,0,),(2,1,),(3,0,),(3,1,),),(),),("front",3,((2,0,),(3,0,),),"s",),("back",3,((0,0,),(1,0,),),(),),("front",3,((0,1,),(1,1,),),"s",),("back",3,((2,0,),(3,0,),),((3,0,),(3,1,),),),("front",3,((2,1,),),"s",),("back",3,((0,1,),(1,1,),),(),),("front",3,((3,1,),),"v",),("back",3,((2,1,),),(),),("out",1,0,"s",),("back",3,((3,1,),),((3,0,),(3,1,),),),("quant",1,(0,),),("mm",0,0,0,0,),("mm",1,0,0,0,),("mm",0,0,1,0,),("mm",1,0,1,0,),("mm",0,1,0,1,),("mm",0,1,1,2,),("out",1,1,"v",),("gelu",0,0,0,),("gelu",0,1,0,),("store",0,),("quant",1,(1,),),("mm",1,1,0,1,),("mm",1,1,1,2,),("gelu",1,0,1,),("gelu",1,1,2,),("store",1,),)
+
+
+def tile_picked_bag_lin_gelu_sub_l_kernel(tc, xT, w_words, w_scales, b, gate, offs, out):
+    nc = tc.nc
+    with ExitStack() as ctx:
+        keep = ctx.enter_context(tc.tile_pool(name="keep", bufs=1))
+        ring = ctx.enter_context(tc.tile_pool(name="ring", bufs=4))
+        psum = ctx.enter_context(tc.psum_pool(name="psum", bufs=1))
+
+        offsets = keep.tile([P, D * V // 16], U16, name="offsets")
+        vec_rows = keep.tile([P, V], F32, name="vec_rows")
+        nc.vector.memset(vec_rows[:], 0.0)
+
+        raw = {}
+        for s in range(2 * PASSES):
+            a, u = divmod(s, 2)
+            rows = xT[512 * a : 512 * (a + 1), :].rearrange("(p t) c -> p t c", t=4)
+            for c0, c1 in zip(LOADS[s][:-1], LOADS[s][1:]):
+                raw[s, c0] = keep.tile([P, 2, c1 - c0], F32, name="raw%d_%d" % (s, c0))
+                nc.sync.dma_start(raw[s, c0][:], rows[:, 2 * u : 2 * u + 2, c0:c1])
+                if s == 0 and c0 == 0:
+                    nc.sync.dma_start(offsets[:], offs)
+                    nc.sync.dma_start(vec_rows[0:D, :], gate[:, 0, :])
+                    nc.sync.dma_start(vec_rows[D : D + 1, :], b.rearrange("m o -> o m"))
+
+        ident = keep.tile([P, P], F32, name="ident")
+        make_identity(nc, ident[:])
+
+        warm = keep.tile([P, 8], F32, name="warm")
+        nc.vector.memset(warm[:], 0.0)
+        warm2 = keep.tile([P, 8], F32, name="warm2")
+        nc.scalar.activation(warm2[:], warm[:], ACT.Gelu_apprx_tanh)
+        vec_ps = psum.tile([P, VB, P], F32, name="vec_ps", tag="fwd", bufs=3)
+        for h in range(VB):
+            nc.tensor.transpose(vec_ps[:, h, :], vec_rows[:, h * P : (h + 1) * P], ident[:])
+        vec = keep.tile([P, VB, 8], F32, name="vec")
+        nc.scalar.copy(vec[:], vec_ps[:, :, 0:8])
+
+        w_codes = keep.tile([P, PASSES, N], U32, name="w_codes", align_bytes=64)
+        w_plane = keep.tile([P, PASSES, N], U8, name="w_plane", align_bytes=64)
+        nc.vector.memset(w_plane[:].rearrange("p a m -> p (a m)").bitcast(I32), 0)
+        nc.sync.dma_start(w_codes[:].bitcast(I32), w_words.rearrange("a p m r -> p a (m r)").bitcast(I32))
+        for q in range(4):
+            nc.sync.dma_start(
+                w_plane[32 * q : 32 * q + 4, :, :].bitcast(I32),
+                w_scales[:, 4 * q : 4 * q + 4, :].rearrange("a r m -> r a m").bitcast(I32),
+            )
+
+        pairs = [keep.tile([P, 2 * T], BF16, name="pairs%d" % s) for s in range(2 * PASSES)]
+        grouped = [keep.tile([P, V, 4], BF16, name="grouped%d" % a, align_bytes=64) for a in range(PASSES)]
+        x_codes = {}
+        x_plane = {}
+        acc = {}
+        seen = {}
+        scaled = {}
+        result = {}
+        final = [keep.tile([P, MB, P], F32, name="final%d" % vb) for vb in range(VB)]
+
+        def cast(s, c0, c1, eng):
+            base = max(c for c in LOADS[s] if c <= c0)
+            dst = pairs[s][:, 2 * c0 : 2 * c1].rearrange("p (c e) -> p c e", e=2)
+            src = raw[s, base][:, :, c0 - base : c1 - base].rearrange("p e c -> p c e")
+            if eng == "v":
+                nc.vector.tensor_copy(dst, src)
+            elif eng == "s":
+                nc.scalar.copy(dst, src)
+            else:
+                nc.gpsimd.tensor_scalar(dst, src, 1.0, 0.0, ALU.mult, ALU.add)
+
+        def front(s, pieces, eng):
+            n = len(pieces)
+            picked = ring.tile([P, n * P], U32, name="picked")
+            j = 0
+            while j < n:
+                first = 2 * pieces[j][0] + pieces[j][1]
+                run = 1
+                while j + run < n and 2 * pieces[j + run][0] + pieces[j + run][1] == first + run:
+                    run += 1
+                nc.vector.tensor_copy(
+                    picked[:, j * P : (j + run) * P],
+                    pairs[s][:].bitcast(U32).indirect(offsets[:, 8 * first : 8 * (first + run)]),
+                )
+                j += run
+            turned = psum.tile([P, n, P], F32, name="turned", tag="fwd", bufs=3)
+            for j in range(n):
+                nc.tensor.transpose(turned[:, j, :], picked[:, j * P : (j + 1) * P].bitcast(F32), ident[:])
+            tile = ring.tile([P, n, 2, P], F32, name="scaled")
+            for j, (d, vb) in enumerate(pieces):
+                src = turned[:, j, :].bitcast(BF16).rearrange("v (p e) -> v e p", e=2)
+                weight = vec[:, vb, d : d + 1]
+                if eng == "s":
+                    nc.scalar.activation(tile[:, j, :, :], src, ACT.Copy, scale=weight)
+                elif eng == "v":
+                    nc.vector.tensor_scalar(tile[:, j, :, :], src, weight, None, ALU.mult)
+                else:
+                    nc.vector.scalar_tensor_tensor(tile[:, j, :, :], src, weight, scaled[s, d - 1, vb], ALU.mult, ALU.add)
+                scaled[s, d, vb] = tile[:, j, :, :]
+
+        def back(s, pieces, last):
+            a, u = divmod(s, 2)
+            for d, vb in pieces:
+                if (a, vb) not in acc:
+                    acc[a, vb] = psum.tile([P, 4, P], F32, name="acc", tag="sum", bufs=5)
+                    seen[a, vb] = 0
+                for e in range(2):
+                    nc.tensor.matmul(
+                        acc[a, vb][:, 2 * u + e, :],
+                        lhsT=scaled[s, d, vb][:, e, :],
+                        rhs=ident[:],
+                        start=(seen[a, vb] == 0),
+                        stop=((d, vb) in last and e == 1),
+                        is_transpose=True,
+                    )
+                    seen[a, vb] += 1
+
+        def gather_out(a, vb, eng):
+            src = acc[a, vb][:].rearrange("p t v -> p v t")
+            if eng == "s":
+                nc.scalar.copy(grouped[a][:, vb * P : (vb + 1) * P, :], src)
+            else:
+                nc.vector.tensor_copy(grouped[a][:, vb * P : (vb + 1) * P, :], src)
+
+        def quant(a, vbs):
+            n = len(vbs) * P
+            codes = keep.tile([P, n], U32, name="x_codes%d_%d" % (a, vbs[0]), align_bytes=64)
+            plane = keep.tile([P, n], U8, name="x_plane%d_%d" % (a, vbs[0]), align_bytes=64)
+            src = grouped[a][:, vbs[0] * P : vbs[0] * P + n, :]
+            nc.vector.quantize_mx(codes[:].bitcast(FP8X4), plane[:], src.rearrange("p v t -> p (v t)"))
+            for i, vb in enumerate(vbs):
+                x_codes[a, vb] = codes[:, i * P : (i + 1) * P]
+                x_plane[a, vb] = plane[:, i * P : (i + 1) * P]
+
+        def product(a, vb, m, bank):
+            if bank not in result:
+                result[bank] = psum.tile([P, MB, P], F32, name="result", tag="sum", bufs=5)
+            cols = slice(m * P, (m + 1) * P)
+            nc.tensor.matmul_mx(
+                result[bank][:, m, :],
+                lhsT=w_codes[:, a, cols].bitcast(FP8X4),
+                lhsT_scale=w_plane[:, a, cols],
+                rhs=x_codes[a, vb].bitcast(FP8X4),
+                rhs_scale=x_plane[a, vb],
+                start=(a == 0),
+                stop=(a == PASSES - 1),
+            )
+
+        def gelu(vb, m, bank):
+            nc.scalar.activation(final[vb][:, m, :], result[bank][:, m, :], ACT.Gelu_apprx_tanh, bias=vec[:, m, D : D + 1])
+
+        def store(vb):
+            nc.sync.dma_start(out[:, vb * P : (vb + 1) * P].rearrange("(m p) v -> p m v", p=P), final[vb][:])
+
+        steps = {"cast": cast, "front": front, "back": back, "out": gather_out, "quant": quant, "mm": product, "gelu": gelu, "store": store}
+        for step in PLAN:
+            steps[step[0]](*step[1:])

@@ -20,32 +20,54 @@ P = 128
 PASSES = K // 512
 VB = V // P
 MB = N // P
-LOADS = ((0,512,768,1024,),(0,512,1024,),(0,512,1024,),(0,512,1024,),)
-PLAN = (("cast",0,0,512,"v",),("cast",0,512,768,"v",),("cast",0,768,1024,"v",),("cast",1,0,512,"s",),("cast",1,512,1024,"g",),("cast",2,0,512,"g",),("cast",2,512,768,"g",),("front",0,((0,0,),(0,1,),),"s",),("front",0,((1,0,),(1,1,),),"s",),("back",0,((0,0,),(0,1,),),(),),("front",0,((2,0,),(2,1,),(3,0,),(3,1,),),"s",),("back",0,((1,0,),(1,1,),),(),),("front",1,((0,0,),(0,1,),(1,0,),(1,1,),),"s",),("back",0,((2,0,),(2,1,),(3,0,),(3,1,),),(),),("front",1,((2,0,),(2,1,),(3,0,),(3,1,),),"s",),("back",1,((0,0,),(0,1,),(1,0,),(1,1,),),(),),("cast",2,768,1024,"v",),("cast",3,0,512,"g",),("cast",3,512,1024,"g",),("front",2,((0,0,),(0,1,),(1,0,),(1,1,),),"s",),("back",1,((2,0,),(2,1,),(3,0,),(3,1,),),((3,0,),(3,1,),),),("front",2,((2,0,),(2,1,),(3,0,),(3,1,),),"s",),("back",2,((0,0,),(0,1,),(1,0,),(1,1,),),(),),("out",0,0,"v",),("out",0,1,"v",),("quant",0,(0,1,),),("front",3,((0,0,),(1,0,),),"s",),("back",2,((2,0,),(2,1,),(3,0,),(3,1,),),(),),("front",3,((2,0,),(3,0,),),"s",),("back",3,((0,0,),(1,0,),),(),),("front",3,((0,1,),(1,1,),),"s",),("back",3,((2,0,),(3,0,),),((3,0,),(3,1,),),),("front",3,((2,1,),),"s",),("back",3,((0,1,),(1,1,),),(),),("front",3,((3,1,),),"v",),("back",3,((2,1,),),(),),("out",1,0,"s",),("back",3,((3,1,),),((3,0,),(3,1,),),),("quant",1,(0,),),("mm",0,0,0,0,),("mm",1,0,0,0,),("mm",0,0,1,0,),("mm",1,0,1,0,),("mm",0,1,0,1,),("mm",0,1,1,2,),("out",1,1,"v",),("gelu",0,0,0,),("gelu",0,1,0,),("store",0,),("quant",1,(1,),),("mm",1,1,0,1,),("mm",1,1,1,2,),("gelu",1,0,1,),("gelu",1,1,2,),("store",1,),)
+LOADS = (("plane",2,0,),("gate",0,),("offs",),("gate",1,),("gate",2,),("gate",3,),("plane",2,1,),("pair",0,0,384,),("pair",0,384,768,),("pair",0,768,1024,),("pair",1,0,512,),("pair",1,512,1024,),("plane",3,0,),("plane",3,1,),)
+BORDERS = ((0,384,768,1024,),(0,512,1024,),(),(),)
+PLAN = (("cast",0,0,384,"s",),("cast",0,384,512,"v",),("cast",1,640,1024,"s",),("cast",0,512,768,"s",),("cast",0,768,1024,"s",),("frontm",2,0,((1,0,),(1,1,),),),("frontm",2,0,((2,0,),(2,1,),(3,0,),(3,1,),),),("cast",1,512,640,"v",),("frontm",2,0,((0,0,),(0,1,),),),("frontm",2,1,((2,0,),(2,1,),(3,0,),(3,1,),),),("cast",1,0,512,"s",),("frontm",2,1,((0,0,),(0,1,),(1,0,),(1,1,),),),("front",0,((0,0,),(0,1,),(1,0,),(1,1,),),"ssss",),("front",0,((2,0,),(2,1,),(3,0,),(3,1,),),"ssss",),("back",0,((0,0,),(0,1,),(1,0,),(1,1,),),),("frontm",3,0,((0,0,),(0,1,),(1,0,),(1,1,),),),("front",1,((2,0,),(2,1,),(3,0,),(3,1,),),"ssss",),("back",0,((2,0,),(2,1,),(3,0,),(3,1,),),),("front",1,((0,0,),(0,1,),(1,0,),(1,1,),),"ssas",),("back",1,((2,0,),(2,1,),(3,0,),(3,1,),),),("midout",2,1,"s",),("frontm",3,1,((2,0,),(3,0,),),),("frontm",3,0,((2,0,),(2,1,),(3,0,),(3,1,),),),("frontm",3,1,((0,0,),(1,0,),),),("back",1,((0,0,),(0,1,),(1,0,),(1,1,),),),("midout",3,0,"s",),("frontm",3,1,((0,1,),(1,1,),),),("midout",2,0,"s",),("out",0,1,"v",),("frontm",3,1,((2,1,),(3,1,),),),("out",0,0,"s",),("midout",3,1,"s",),("quant",0,(0,1,),),("backw",2,0,),("backw",3,0,),("backw",2,1,),("backw",3,1,),("mm",0,1,0,1,),("out",1,1,"s",),("mm",0,0,0,0,),("out",1,0,"s",),("quant",1,(0,),),("mm",1,0,0,0,),("mm",0,0,1,0,),("mm",1,0,1,0,),("quant",1,(1,),),("mm",0,1,1,2,),("mm",1,1,1,2,),("gelu",0,0,0,),("gelu",1,1,2,),("mm",1,1,0,1,),("gelu",0,1,0,),("gelu",1,0,1,),("store",0,),("store",1,),)
 
 
 def tile_picked_bag_lin_gelu_sub_l_kernel(tc, xT, w_words, w_scales, b, gate, offs, out):
     nc = tc.nc
     with ExitStack() as ctx:
         keep = ctx.enter_context(tc.tile_pool(name="keep", bufs=1))
-        ring = ctx.enter_context(tc.tile_pool(name="ring", bufs=4))
         psum = ctx.enter_context(tc.psum_pool(name="psum", bufs=1))
+        free_banks = list(range(8))
+        bank_of = {}
+        banks = [psum.tile([P, 4 * P], F32, name="bank%d" % i) for i in range(8)]
+        ring = [keep.tile([P, 4 * P], U32, name="ring%d" % i) for i in range(3)]
+        turns = []
+
+        def next_slot():
+            turns.append(0)
+            return ring[(len(turns) - 1) % len(ring)]
+
+        def take(key, shape):
+            bank_of[key] = free_banks.pop(0)
+            return banks[bank_of[key]][:, 0 : shape[1] * P].rearrange("p (j c) -> p j c", c=P)
+
+        def give(key):
+            free_banks.append(bank_of[key])
 
         offsets = keep.tile([P, D * V // 16], U16, name="offsets")
         vec_rows = keep.tile([P, V], F32, name="vec_rows")
-        nc.vector.memset(vec_rows[:], 0.0)
+        nc.gpsimd.memset(vec_rows[:], 0.0)
+        nc.sync.dma_start(vec_rows[0:D, :], gate[:, 0, :])
+        gate_k = keep.tile([P, D * V], F32, name="gate_k")
 
         raw = {}
-        for s in range(2 * PASSES):
-            a, u = divmod(s, 2)
-            rows = xT[512 * a : 512 * (a + 1), :].rearrange("(p t) c -> p t c", t=4)
-            for c0, c1 in zip(LOADS[s][:-1], LOADS[s][1:]):
-                raw[s, c0] = keep.tile([P, 2, c1 - c0], F32, name="raw%d_%d" % (s, c0))
-                nc.sync.dma_start(raw[s, c0][:], rows[:, 2 * u : 2 * u + 2, c0:c1])
-                if s == 0 and c0 == 0:
-                    nc.sync.dma_start(offsets[:], offs)
-                    nc.sync.dma_start(vec_rows[0:D, :], gate[:, 0, :])
-                    nc.sync.dma_start(vec_rows[D : D + 1, :], b.rearrange("m o -> o m"))
+        for item in LOADS:
+            if item[0] == "offs":
+                nc.sync.dma_start(offsets[:], offs)
+            elif item[0] == "gate":
+                nc.sync.dma_start(gate_k[:, item[1] * V : (item[1] + 1) * V], gate[item[1]])
+            else:
+                a, u = divmod(item[1], 2)
+                rows = xT[512 * a : 512 * (a + 1), :].rearrange("(p t) c -> p t c", t=4)
+                if item[0] == "plane":
+                    raw[item] = keep.tile([P, T], F32, name="plane%d_%d" % item[1:])
+                    nc.sync.dma_start(raw[item][:], rows[:, 2 * u + item[2], :])
+                else:
+                    raw[item[:3]] = keep.tile([P, 2, item[3] - item[2]], F32, name="raw%d_%d" % item[1:3])
+                    nc.sync.dma_start(raw[item[:3]][:], rows[:, 2 * u : 2 * u + 2, item[2] : item[3]])
 
         ident = keep.tile([P, P], F32, name="ident")
         make_identity(nc, ident[:])
@@ -54,95 +76,168 @@ def tile_picked_bag_lin_gelu_sub_l_kernel(tc, xT, w_words, w_scales, b, gate, of
         nc.vector.memset(warm[:], 0.0)
         warm2 = keep.tile([P, 8], F32, name="warm2")
         nc.scalar.activation(warm2[:], warm[:], ACT.Gelu_apprx_tanh)
-        vec_ps = psum.tile([P, VB, P], F32, name="vec_ps", tag="fwd", bufs=3)
+        vec_ps = take("vec", [P, VB, P])
         for h in range(VB):
             nc.tensor.transpose(vec_ps[:, h, :], vec_rows[:, h * P : (h + 1) * P], ident[:])
         vec = keep.tile([P, VB, 8], F32, name="vec")
         nc.scalar.copy(vec[:], vec_ps[:, :, 0:8])
+        give("vec")
 
         w_codes = keep.tile([P, PASSES, N], U32, name="w_codes", align_bytes=64)
         w_plane = keep.tile([P, PASSES, N], U8, name="w_plane", align_bytes=64)
         nc.vector.memset(w_plane[:].rearrange("p a m -> p (a m)").bitcast(I32), 0)
         nc.sync.dma_start(w_codes[:].bitcast(I32), w_words.rearrange("a p m r -> p a (m r)").bitcast(I32))
+        bias = keep.tile([P, MB], F32, name="bias")
+        with nc.allow_non_contiguous_dma(reason="one bias value a partition"):
+            nc.sync.dma_start(bias[:], b.rearrange("(m p) o -> p (m o)", p=P))
         for q in range(4):
             nc.sync.dma_start(
                 w_plane[32 * q : 32 * q + 4, :, :].bitcast(I32),
                 w_scales[:, 4 * q : 4 * q + 4, :].rearrange("a r m -> r a m").bitcast(I32),
             )
 
-        pairs = [keep.tile([P, 2 * T], BF16, name="pairs%d" % s) for s in range(2 * PASSES)]
+        pairs = {}
         grouped = [keep.tile([P, V, 4], BF16, name="grouped%d" % a, align_bytes=64) for a in range(PASSES)]
         x_codes = {}
         x_plane = {}
         acc = {}
-        seen = {}
+        summed = {}
         scaled = {}
+        mid = {}
+        words = {}
+        as_words = set()
         result = {}
+        count = [0]
         final = [keep.tile([P, MB, P], F32, name="final%d" % vb) for vb in range(VB)]
 
-        def cast(s, c0, c1, eng):
-            base = max(c for c in LOADS[s] if c <= c0)
-            dst = pairs[s][:, 2 * c0 : 2 * c1].rearrange("p (c e) -> p c e", e=2)
-            src = raw[s, base][:, :, c0 - base : c1 - base].rearrange("p e c -> p c e")
-            if eng == "v":
-                nc.vector.tensor_copy(dst, src)
-            elif eng == "s":
+        def fresh(stem, shape, dtype):
+            count.append(0)
+            return keep.tile(shape, dtype, name="%s%d" % (stem, len(count)))
+
+        def runs(pieces):
+            found = []
+            for j, (d, vb) in enumerate(pieces):
+                if found and found[-1][1] + found[-1][2] == 2 * d + vb:
+                    found[-1] = (found[-1][0], found[-1][1], found[-1][2] + 1)
+                else:
+                    found.append((j, 2 * d + vb, 1))
+            return found
+
+        def copy(eng, dst, src):
+            if eng == "s":
                 nc.scalar.copy(dst, src)
             else:
-                nc.gpsimd.tensor_scalar(dst, src, 1.0, 0.0, ALU.mult, ALU.add)
+                nc.vector.tensor_copy(dst, src)
 
-        def front(s, pieces, eng):
+        def gate_spread(ds):
+            spread = take("gate", [P, 2 * len(ds), P])
+            for i, d in enumerate(ds):
+                for vb in range(VB):
+                    nc.tensor.transpose(spread[:, 2 * i + vb, :], vec[:, vb, d : d + 1].to_broadcast([P, P]), ident[:])
+            nc.scalar.copy(gate_k[:, ds[0] * V : (ds[-1] + 1) * V], spread.rearrange("p j v -> p (j v)"))
+            give("gate")
+
+        def cast(s, c0, c1, eng):
+            if s not in pairs:
+                pairs[s] = keep.tile([P, 2 * T], BF16, name="pairs%d" % s)
+            base = max(c for c in BORDERS[s] if c <= c0)
+            dst = pairs[s][:, 2 * c0 : 2 * c1].rearrange("p (c e) -> p c e", e=2)
+            src = raw["pair", s, base][:, :, c0 - base : c1 - base].rearrange("p e c -> p c e")
+            if eng == "g":
+                nc.gpsimd.tensor_scalar(dst, src, 1.0, 0.0, ALU.mult, ALU.add)
+            else:
+                copy(eng, dst, src)
+
+        def front(s, pieces, engs):
             n = len(pieces)
-            picked = ring.tile([P, n * P], U32, name="picked")
-            j = 0
-            while j < n:
-                first = 2 * pieces[j][0] + pieces[j][1]
-                run = 1
-                while j + run < n and 2 * pieces[j + run][0] + pieces[j + run][1] == first + run:
-                    run += 1
+            picked = next_slot()
+            for j, first, run in runs(pieces):
                 nc.vector.tensor_copy(
                     picked[:, j * P : (j + run) * P],
                     pairs[s][:].bitcast(U32).indirect(offsets[:, 8 * first : 8 * (first + run)]),
                 )
-                j += run
-            turned = psum.tile([P, n, P], F32, name="turned", tag="fwd", bufs=3)
+            turned = take("turned", [P, n, P])
             for j in range(n):
                 nc.tensor.transpose(turned[:, j, :], picked[:, j * P : (j + 1) * P].bitcast(F32), ident[:])
-            tile = ring.tile([P, n, 2, P], F32, name="scaled")
+            tile = fresh("scaled", [P, n, 2, P], F32)
             for j, (d, vb) in enumerate(pieces):
                 src = turned[:, j, :].bitcast(BF16).rearrange("v (p e) -> v e p", e=2)
                 weight = vec[:, vb, d : d + 1]
-                if eng == "s":
+                terms = 1
+                if engs[j] == "s":
                     nc.scalar.activation(tile[:, j, :, :], src, ACT.Copy, scale=weight)
-                elif eng == "v":
+                elif engs[j] == "v":
                     nc.vector.tensor_scalar(tile[:, j, :, :], src, weight, None, ALU.mult)
                 else:
-                    nc.vector.scalar_tensor_tensor(tile[:, j, :, :], src, weight, scaled[s, d - 1, vb], ALU.mult, ALU.add)
-                scaled[s, d, vb] = tile[:, j, :, :]
+                    key = [k for k in scaled if k[0] == s and k[2] == vb][-1]
+                    earlier, before = scaled.pop(key)
+                    terms += before
+                    nc.vector.scalar_tensor_tensor(tile[:, j, :, :], src, weight, earlier, ALU.mult, ALU.add)
+                scaled[s, d, vb] = (tile[:, j, :, :], terms)
+            give("turned")
 
-        def back(s, pieces, last):
+        def back(s, pieces):
             a, u = divmod(s, 2)
             for d, vb in pieces:
+                if (s, d, vb) not in scaled:
+                    continue
+                src, terms = scaled.pop((s, d, vb))
                 if (a, vb) not in acc:
-                    acc[a, vb] = psum.tile([P, 4, P], F32, name="acc", tag="sum", bufs=5)
-                    seen[a, vb] = 0
+                    acc[a, vb] = take(("acc", a, vb), [P, 4, P])
+                    summed[a, vb] = 0
                 for e in range(2):
+                    first = summed[a, vb] == 0
+                    summed[a, vb] += terms
                     nc.tensor.matmul(
                         acc[a, vb][:, 2 * u + e, :],
-                        lhsT=scaled[s, d, vb][:, e, :],
+                        lhsT=src[:, e, :],
                         rhs=ident[:],
-                        start=(seen[a, vb] == 0),
-                        stop=((d, vb) in last and e == 1),
+                        start=first,
+                        stop=(summed[a, vb] == 4 * D),
                         is_transpose=True,
                     )
-                    seen[a, vb] += 1
 
-        def gather_out(a, vb, eng):
-            src = acc[a, vb][:].rearrange("p t v -> p v t")
-            if eng == "s":
-                nc.scalar.copy(grouped[a][:, vb * P : (vb + 1) * P, :], src)
-            else:
-                nc.vector.tensor_copy(grouped[a][:, vb * P : (vb + 1) * P, :], src)
+        def front_plain(s, e, pieces):
+            weighted = next_slot()[:].bitcast(F32)
+            for j, first, run in runs(pieces):
+                nc.vector.tensor_tensor(
+                    weighted[:, j * P : (j + run) * P],
+                    raw["plane", s, e][:].indirect(offsets[:, 8 * first : 8 * (first + run)]),
+                    gate_k[:, first * P : (first + run) * P],
+                    ALU.mult,
+                )
+            for j, (d, vb) in enumerate(pieces):
+                if (s, vb) not in mid:
+                    mid[s, vb] = take(("mid", s, vb), [P, 2, P])
+                    summed["mid", s, vb] = 0
+                summed["mid", s, vb] += 1
+                nc.tensor.matmul(
+                    mid[s, vb][:, e, :],
+                    lhsT=weighted[:, j * P : (j + 1) * P],
+                    rhs=ident[:],
+                    start=(summed["mid", s, vb] == 1),
+                    stop=(summed["mid", s, vb] == 2 * D),
+                    is_transpose=True,
+                )
+
+        def mid_out(s, vb, eng):
+            words[s, vb] = fresh("words", [P, P, 2], BF16)
+            copy(eng, words[s, vb][:], mid[s, vb].rearrange("v e p -> v p e"))
+            give(("mid", s, vb))
+
+        def back_words(s, vb):
+            a, u = divmod(s, 2)
+            if (a, vb) not in acc:
+                acc[a, vb] = take(("acc", a, vb), [P, 2, P])
+                as_words.add(a)
+            nc.tensor.transpose(acc[a, vb][:, u, :], words[s, vb][:].rearrange("v p e -> v (p e)").bitcast(F32), ident[:])
+
+        def sums_out(a, vb, eng):
+            dst = grouped[a][:, vb * P : (vb + 1) * P, :]
+            if a in as_words:
+                dst = dst.bitcast(F32)
+            copy(eng, dst, acc[a, vb].rearrange("p t v -> p v t"))
+            give(("acc", a, vb))
 
         def quant(a, vbs):
             n = len(vbs) * P
@@ -156,7 +251,7 @@ def tile_picked_bag_lin_gelu_sub_l_kernel(tc, xT, w_words, w_scales, b, gate, of
 
         def product(a, vb, m, bank):
             if bank not in result:
-                result[bank] = psum.tile([P, MB, P], F32, name="result", tag="sum", bufs=5)
+                result[bank] = take(("result", bank), [P, MB, P])
             cols = slice(m * P, (m + 1) * P)
             nc.tensor.matmul_mx(
                 result[bank][:, m, :],
@@ -169,11 +264,12 @@ def tile_picked_bag_lin_gelu_sub_l_kernel(tc, xT, w_words, w_scales, b, gate, of
             )
 
         def gelu(vb, m, bank):
-            nc.scalar.activation(final[vb][:, m, :], result[bank][:, m, :], ACT.Gelu_apprx_tanh, bias=vec[:, m, D : D + 1])
+            nc.scalar.activation(final[vb][:, m, :], result[bank][:, m, :], ACT.Gelu_apprx_tanh, bias=bias[:, m : m + 1])
 
         def store(vb):
             nc.sync.dma_start(out[:, vb * P : (vb + 1) * P].rearrange("(m p) v -> p m v", p=P), final[vb][:])
 
-        steps = {"cast": cast, "front": front, "back": back, "out": gather_out, "quant": quant, "mm": product, "gelu": gelu, "store": store}
+        steps = {"cast": cast, "front": front, "back": back, "out": sums_out, "quant": quant, "mm": product, "gelu": gelu, "store": store,
+                 "gateb": gate_spread, "frontm": front_plain, "midout": mid_out, "backw": back_words}
         for step in PLAN:
             steps[step[0]](*step[1:])

@@ -1,7 +1,6 @@
 from contextlib import ExitStack
 
 import concourse.mybir as mybir
-from concourse.masks import make_identity
 
 K, T, D, V, N = 1024, 1024, 4, 256, 256
 FLOPS = 2 * K * N * V
@@ -20,9 +19,9 @@ P = 128
 PASSES = K // 512
 VB = V // P
 MB = N // P
-LOADS = (("plane",2,0,),("gate",0,),("offs",),("gate",1,),("gate",2,),("gate",3,),("plane",2,1,),("pair",0,0,384,),("pair",0,384,768,),("pair",0,768,1024,),("pair",1,0,512,),("pair",1,512,1024,),("plane",3,0,),("plane",3,1,),)
-BORDERS = ((0,384,768,1024,),(0,512,1024,),(),(),)
-PLAN = (("cast",0,0,384,"s",),("cast",0,384,512,"v",),("cast",1,640,1024,"s",),("cast",0,512,768,"s",),("cast",0,768,1024,"s",),("frontm",2,0,((1,0,),(1,1,),),),("frontm",2,0,((2,0,),(2,1,),(3,0,),(3,1,),),),("cast",1,512,640,"v",),("frontm",2,0,((0,0,),(0,1,),),),("frontm",2,1,((2,0,),(2,1,),(3,0,),(3,1,),),),("cast",1,0,512,"s",),("frontm",2,1,((0,0,),(0,1,),(1,0,),(1,1,),),),("front",0,((0,0,),(0,1,),(1,0,),(1,1,),),"ssss",),("front",0,((2,0,),(2,1,),(3,0,),(3,1,),),"ssss",),("back",0,((0,0,),(0,1,),(1,0,),(1,1,),),),("frontm",3,0,((0,0,),(0,1,),(1,0,),(1,1,),),),("front",1,((2,0,),(2,1,),(3,0,),(3,1,),),"ssss",),("back",0,((2,0,),(2,1,),(3,0,),(3,1,),),),("front",1,((0,0,),(0,1,),(1,0,),(1,1,),),"ssas",),("back",1,((2,0,),(2,1,),(3,0,),(3,1,),),),("midout",2,1,"s",),("frontm",3,1,((2,0,),(3,0,),),),("frontm",3,0,((2,0,),(2,1,),(3,0,),(3,1,),),),("frontm",3,1,((0,0,),(1,0,),),),("back",1,((0,0,),(0,1,),(1,0,),(1,1,),),),("midout",3,0,"s",),("frontm",3,1,((0,1,),(1,1,),),),("midout",2,0,"s",),("out",0,1,"v",),("frontm",3,1,((2,1,),(3,1,),),),("out",0,0,"s",),("midout",3,1,"s",),("quant",0,(0,1,),),("backw",2,0,),("backw",3,0,),("backw",2,1,),("backw",3,1,),("mm",0,1,0,1,),("out",1,1,"s",),("mm",0,0,0,0,),("out",1,0,"s",),("quant",1,(0,),),("mm",1,0,0,0,),("mm",0,0,1,0,),("mm",1,0,1,0,),("quant",1,(1,),),("mm",0,1,1,2,),("mm",1,1,1,2,),("gelu",0,0,0,),("gelu",1,1,2,),("mm",1,1,0,1,),("gelu",0,1,0,),("gelu",1,0,1,),("store",0,),("store",1,),)
+LOADS = (("pair",0,0,512,),("offs",),("pair",0,512,768,),("pair",0,768,1024,),("pair",1,0,384,),("pair",1,384,768,),("pair",1,768,1024,),("pair",2,0,512,),("pair",2,512,1024,),("pair",3,0,512,),("pair",3,512,1024,),)
+BORDERS = ((0,512,768,1024,),(0,384,768,1024,),(0,512,1024,),(0,512,1024,),)
+PLAN = (("cast",0,896,1024,"s",),("cast",0,768,896,"v",),("cast",0,512,640,"v",),("cast",0,640,768,"s",),("cast",1,768,1024,"v",),("cast",2,0,256,"s",),("cast",0,384,512,"v",),("cast",3,512,640,"s",),("cast",2,512,1024,"s",),("cast",0,0,256,"v",),("cast",0,256,384,"s",),("cast",2,256,384,"v",),("cast",2,384,512,"s",),("front",0,((1,0,),(1,1,),),"ss",),("cast",1,0,384,"s",),("cast",1,512,768,"s",),("front",0,((2,0,),(2,1,),(3,0,),(3,1,),),"ssss",),("back",0,((2,0,),(2,1,),(3,0,),(3,1,),),),("front",0,((0,0,),(0,1,),),"ss",),("cast",1,384,512,"v",),("front",1,((2,0,),(2,1,),(3,0,),(3,1,),),"ssss",),("cast",3,0,512,"v",),("back",0,((0,0,),(0,1,),(1,0,),(1,1,),),),("front",1,((0,0,),(0,1,),(1,0,),(1,1,),),"saaa",),("cast",3,768,1024,"s",),("cast",3,640,768,"s",),("back",1,((2,0,),(2,1,),(3,0,),(3,1,),),),("front",2,((0,0,),(0,1,),(1,0,),(1,1,),),"ssss",),("front",3,((0,0,),(1,0,),),"sa",),("front",2,((2,0,),(2,1,),(3,0,),(3,1,),),"ssss",),("back",1,((0,0,),(0,1,),(1,0,),(1,1,),),),("back",2,((0,0,),(0,1,),(1,0,),(1,1,),),),("front",3,((0,1,),(1,1,),),"ss",),("out",0,0,"s",),("front",3,((2,0,),(3,0,),),"aa",),("front",3,((3,1,),),"a",),("front",3,((2,1,),),"a",),("out",0,1,"s",),("back",2,((2,0,),(2,1,),(3,0,),(3,1,),),),("back",3,((0,0,),(1,0,),(2,0,),(3,0,),),),("quant",0,(0,1,),),("out",1,0,"s",),("mm",0,1,0,1,),("quant",1,(0,),),("back",3,((0,1,),(1,1,),(2,1,),(3,1,),),),("out",1,1,"s",),("mm",0,0,0,0,),("mm",1,0,0,0,),("mm",0,0,1,0,),("mm",0,1,1,2,),("mm",1,0,1,0,),("quant",1,(1,),),("mm",1,1,0,1,),("gelu",1,0,1,),("mm",1,1,1,2,),("gelu",0,0,0,),("gelu",1,1,2,),("gelu",0,1,0,),("store",0,),("store",1,),)
 
 
 def tile_picked_bag_lin_gelu_sub_l_kernel(tc, xT, w_words, w_scales, b, gate, offs, out):
@@ -49,7 +48,7 @@ def tile_picked_bag_lin_gelu_sub_l_kernel(tc, xT, w_words, w_scales, b, gate, of
 
         offsets = keep.tile([P, D * V // 16], U16, name="offsets")
         vec_rows = keep.tile([P, V], F32, name="vec_rows")
-        nc.gpsimd.memset(vec_rows[:], 0.0)
+        nc.vector.memset(vec_rows[:], 0.0)
         nc.sync.dma_start(vec_rows[0:D, :], gate[:, 0, :])
         gate_k = keep.tile([P, D * V], F32, name="gate_k")
 
@@ -70,7 +69,16 @@ def tile_picked_bag_lin_gelu_sub_l_kernel(tc, xT, w_words, w_scales, b, gate, of
                     nc.sync.dma_start(raw[item[:3]][:], rows[:, 2 * u : 2 * u + 2, item[2] : item[3]])
 
         ident = keep.tile([P, P], F32, name="ident")
-        make_identity(nc, ident[:])
+        ones = keep.tile([P, P], F32, name="ones")
+        column = keep.tile([P, P], F32, name="column", align_bytes=64)
+        in_quadrant = keep.tile([P, 32], F32, name="in_quadrant", align_bytes=64)
+        quadrant = keep.tile([P, 1], F32, name="quadrant")
+        nc.vector.memset(ones[:], 1.0)
+        for q in range(4):
+            nc.vector.memset(quadrant[32 * q : 32 * (q + 1), :], 32.0 * q)
+        nc.vector.tensor_tensor_scan(column[:], ones[:], ones[:], -1.0, ALU.mult, ALU.add)
+        nc.vector.transpose(in_quadrant[:], column[:, 0:32])
+        nc.vector.tensor_scalar(ident[:], column[:], in_quadrant[:, 0:1], quadrant[:], ALU.subtract, ALU.is_equal)
 
         warm = keep.tile([P, 8], F32, name="warm")
         nc.vector.memset(warm[:], 0.0)

@@ -16,12 +16,20 @@ ACT = mybir.ActivationFunctionType
 ALU = mybir.AluOpType
 
 P = 128
-PASSES = K // 512
-VB = V // P
-MB = N // P
-LOADS = (("pair",0,0,512,),("offs",),("pair",0,512,768,),("pair",0,768,1024,),("pair",1,0,384,),("pair",1,384,768,),("pair",1,768,1024,),("pair",2,0,512,),("pair",2,512,1024,),("pair",3,0,512,),("pair",3,512,1024,),)
-BORDERS = ((0,512,768,1024,),(0,384,768,1024,),(0,512,1024,),(0,512,1024,),)
-PLAN = (("cast",0,896,1024,"s",),("cast",0,768,896,"v",),("cast",0,512,640,"v",),("cast",0,640,768,"s",),("cast",1,768,1024,"v",),("cast",2,0,256,"s",),("cast",0,384,512,"v",),("cast",3,512,640,"s",),("cast",2,512,1024,"s",),("cast",0,0,256,"v",),("cast",0,256,384,"s",),("cast",2,256,384,"v",),("cast",2,384,512,"s",),("front",0,((1,0,),(1,1,),),"ss",),("cast",1,0,384,"s",),("cast",1,512,768,"s",),("front",0,((2,0,),(2,1,),(3,0,),(3,1,),),"ssss",),("back",0,((2,0,),(2,1,),(3,0,),(3,1,),),),("front",0,((0,0,),(0,1,),),"ss",),("cast",1,384,512,"v",),("front",1,((2,0,),(2,1,),(3,0,),(3,1,),),"ssss",),("cast",3,0,512,"v",),("back",0,((0,0,),(0,1,),(1,0,),(1,1,),),),("front",1,((0,0,),(0,1,),(1,0,),(1,1,),),"saaa",),("cast",3,768,1024,"s",),("cast",3,640,768,"s",),("back",1,((2,0,),(2,1,),(3,0,),(3,1,),),),("front",2,((0,0,),(0,1,),(1,0,),(1,1,),),"ssss",),("front",3,((0,0,),(1,0,),),"sa",),("front",2,((2,0,),(2,1,),(3,0,),(3,1,),),"ssss",),("back",1,((0,0,),(0,1,),(1,0,),(1,1,),),),("back",2,((0,0,),(0,1,),(1,0,),(1,1,),),),("front",3,((0,1,),(1,1,),),"ss",),("out",0,0,"s",),("front",3,((2,0,),(3,0,),),"aa",),("front",3,((3,1,),),"a",),("front",3,((2,1,),),"a",),("out",0,1,"s",),("back",2,((2,0,),(2,1,),(3,0,),(3,1,),),),("back",3,((0,0,),(1,0,),(2,0,),(3,0,),),),("quant",0,(0,1,),),("out",1,0,"s",),("mm",0,1,0,1,),("quant",1,(0,),),("back",3,((0,1,),(1,1,),(2,1,),(3,1,),),),("out",1,1,"s",),("mm",0,0,0,0,),("mm",1,0,0,0,),("mm",0,0,1,0,),("mm",0,1,1,2,),("mm",1,0,1,0,),("quant",1,(1,),),("mm",1,1,0,1,),("gelu",1,0,1,),("mm",1,1,1,2,),("gelu",0,0,0,),("gelu",1,1,2,),("gelu",0,1,0,),("store",0,),("store",1,),)
+PACK = 4
+K_PASS = P * PACK
+PASSES = K // K_PASS
+HALVES = V // P
+M_BLOCKS = N // P
+QUAD = 32
+BANK = 512
+CHUNK = T // 2
+SPLIT = 128
+LIST_COLS = P // 16
+GATE_COLS = 8
+
+LOW = ((0, 0), (0, 1), (1, 0), (1, 1))
+HIGH = ((2, 0), (2, 1), (3, 0), (3, 1))
 
 
 def tile_picked_bag_lin_gelu_sub_l_kernel(tc, xT, w_words, w_scales, b, gate, offs, out):
@@ -29,255 +37,251 @@ def tile_picked_bag_lin_gelu_sub_l_kernel(tc, xT, w_words, w_scales, b, gate, of
     with ExitStack() as ctx:
         keep = ctx.enter_context(tc.tile_pool(name="keep", bufs=1))
         psum = ctx.enter_context(tc.psum_pool(name="psum", bufs=1))
-        free_banks = list(range(8))
-        bank_of = {}
-        banks = [psum.tile([P, 4 * P], F32, name="bank%d" % i) for i in range(8)]
+        banks = [psum.tile([P, BANK], F32, name="bank%d" % i) for i in range(8)]
         ring = [keep.tile([P, 4 * P], U32, name="ring%d" % i) for i in range(3)]
-        turns = []
 
-        def next_slot():
-            turns.append(0)
-            return ring[(len(turns) - 1) % len(ring)]
-
-        def take(key, shape):
-            bank_of[key] = free_banks.pop(0)
-            return banks[bank_of[key]][:, 0 : shape[1] * P].rearrange("p (j c) -> p j c", c=P)
-
-        def give(key):
-            free_banks.append(bank_of[key])
+        def blocks(bank, n):
+            return banks[bank][:, 0 : n * P].rearrange("p (j c) -> p j c", c=P)
 
         offsets = keep.tile([P, D * V // 16], U16, name="offsets")
-        vec_rows = keep.tile([P, V], F32, name="vec_rows")
-        nc.vector.memset(vec_rows[:], 0.0)
-        nc.sync.dma_start(vec_rows[0:D, :], gate[:, 0, :])
-        gate_k = keep.tile([P, D * V], F32, name="gate_k")
+        gate_rows = keep.tile([P, V], F32, name="gate_rows")
+        nc.vector.memset(gate_rows[:], 0.0)
+        nc.sync.dma_start(gate_rows[0:D, :], gate[:, 0, :])
+        gate_wide = keep.tile([P, D * V], F32, name="gate_wide")
+        planes = {}
+        chunks = {}
 
-        raw = {}
-        for item in LOADS:
-            if item[0] == "offs":
-                nc.sync.dma_start(offsets[:], offs)
-            elif item[0] == "gate":
-                nc.sync.dma_start(gate_k[:, item[1] * V : (item[1] + 1) * V], gate[item[1]])
-            else:
-                a, u = divmod(item[1], 2)
-                rows = xT[512 * a : 512 * (a + 1), :].rearrange("(p t) c -> p t c", t=4)
-                if item[0] == "plane":
-                    raw[item] = keep.tile([P, T], F32, name="plane%d_%d" % item[1:])
-                    nc.sync.dma_start(raw[item][:], rows[:, 2 * u + item[2], :])
-                else:
-                    raw[item[:3]] = keep.tile([P, 2, item[3] - item[2]], F32, name="raw%d_%d" % item[1:3])
-                    nc.sync.dma_start(raw[item[:3]][:], rows[:, 2 * u : 2 * u + 2, item[2] : item[3]])
+        def pass_rows(a):
+            return xT[K_PASS * a : K_PASS * (a + 1), :].rearrange("(p t) c -> p t c", t=PACK)
+
+        def load_plane(s, e):
+            planes[s, e] = keep.tile([P, T], F32, name="plane%d_%d" % (s, e))
+            nc.sync.dma_start(planes[s, e][:], pass_rows(s // 2)[:, 2 * (s % 2) + e, :])
+
+        load_plane(2, 0)
+        nc.sync.dma_start(gate_wide[:, 0:V], gate[0])
+        nc.sync.dma_start(offsets[:], offs)
+        nc.sync.dma_start(gate_wide[:, V : 2 * V], gate[1])
+        load_plane(2, 1)
+        for s in range(2):
+            for c in range(T // CHUNK):
+                chunks[s, c] = keep.tile([P, 2, CHUNK], F32, name="chunk%d_%d" % (s, c))
+                nc.sync.dma_start(chunks[s, c][:], pass_rows(0)[:, 2 * s : 2 * s + 2, c * CHUNK : (c + 1) * CHUNK])
+        load_plane(3, 0)
+        load_plane(3, 1)
 
         ident = keep.tile([P, P], F32, name="ident")
         ones = keep.tile([P, P], F32, name="ones")
         column = keep.tile([P, P], F32, name="column", align_bytes=64)
-        in_quadrant = keep.tile([P, 32], F32, name="in_quadrant", align_bytes=64)
+        in_quadrant = keep.tile([P, QUAD], F32, name="in_quadrant", align_bytes=64)
         quadrant = keep.tile([P, 1], F32, name="quadrant")
         nc.vector.memset(ones[:], 1.0)
-        for q in range(4):
-            nc.vector.memset(quadrant[32 * q : 32 * (q + 1), :], 32.0 * q)
+        for q in range(P // QUAD):
+            nc.vector.memset(quadrant[QUAD * q : QUAD * (q + 1), :], float(QUAD * q))
         nc.vector.tensor_tensor_scan(column[:], ones[:], ones[:], -1.0, ALU.mult, ALU.add)
-        nc.vector.transpose(in_quadrant[:], column[:, 0:32])
+        nc.vector.transpose(in_quadrant[:], column[:, 0:QUAD])
         nc.vector.tensor_scalar(ident[:], column[:], in_quadrant[:, 0:1], quadrant[:], ALU.subtract, ALU.is_equal)
 
-        warm = keep.tile([P, 8], F32, name="warm")
-        nc.vector.memset(warm[:], 0.0)
-        warm2 = keep.tile([P, 8], F32, name="warm2")
-        nc.scalar.activation(warm2[:], warm[:], ACT.Gelu_apprx_tanh)
-        vec_ps = take("vec", [P, VB, P])
-        for h in range(VB):
-            nc.tensor.transpose(vec_ps[:, h, :], vec_rows[:, h * P : (h + 1) * P], ident[:])
-        vec = keep.tile([P, VB, 8], F32, name="vec")
-        nc.scalar.copy(vec[:], vec_ps[:, :, 0:8])
-        give("vec")
+        warm_in = keep.tile([P, 8], F32, name="warm_in")
+        nc.vector.memset(warm_in[:], 0.0)
+        warm_out = keep.tile([P, 8], F32, name="warm_out")
+        nc.scalar.activation(warm_out[:], warm_in[:], ACT.Gelu_apprx_tanh)
+
+        for h in range(HALVES):
+            nc.tensor.transpose(blocks(0, HALVES)[:, h, :], gate_rows[:, h * P : (h + 1) * P], ident[:])
+        gate_col = keep.tile([P, HALVES, GATE_COLS], F32, name="gate_col")
+        nc.scalar.copy(gate_col[:], blocks(0, HALVES)[:, :, 0:GATE_COLS])
 
         w_codes = keep.tile([P, PASSES, N], U32, name="w_codes", align_bytes=64)
         w_plane = keep.tile([P, PASSES, N], U8, name="w_plane", align_bytes=64)
         nc.vector.memset(w_plane[:].rearrange("p a m -> p (a m)").bitcast(I32), 0)
         nc.sync.dma_start(w_codes[:].bitcast(I32), w_words.rearrange("a p m r -> p a (m r)").bitcast(I32))
-        bias = keep.tile([P, MB], F32, name="bias")
+        bias = keep.tile([P, M_BLOCKS], F32, name="bias")
         with nc.allow_non_contiguous_dma(reason="one bias value a partition"):
             nc.sync.dma_start(bias[:], b.rearrange("(m p) o -> p (m o)", p=P))
-        for q in range(4):
+        for q in range(P // QUAD):
             nc.sync.dma_start(
-                w_plane[32 * q : 32 * q + 4, :, :].bitcast(I32),
+                w_plane[QUAD * q : QUAD * q + 4, :, :].bitcast(I32),
                 w_scales[:, 4 * q : 4 * q + 4, :].rearrange("a r m -> r a m").bitcast(I32),
             )
 
-        pairs = {}
-        grouped = [keep.tile([P, V, 4], BF16, name="grouped%d" % a, align_bytes=64) for a in range(PASSES)]
+        grouped = [keep.tile([P, V, PACK], BF16, name="grouped%d" % a, align_bytes=64) for a in range(PASSES)]
+        final = [keep.tile([P, M_BLOCKS, P], F32, name="final%d" % h) for h in range(HALVES)]
+        pair_words = [keep.tile([P, 2 * T], BF16, name="pair_words%d" % s) for s in range(2)]
+        scaled = {}
+        rounded = {}
         x_codes = {}
         x_plane = {}
-        acc = {}
-        summed = {}
-        scaled = {}
-        mid = {}
-        words = {}
-        as_words = set()
-        result = {}
-        count = [0]
-        final = [keep.tile([P, MB, P], F32, name="final%d" % vb) for vb in range(VB)]
 
-        def fresh(stem, shape, dtype):
-            count.append(0)
-            return keep.tile(shape, dtype, name="%s%d" % (stem, len(count)))
+        bag_sums = {(2, 0): blocks(7, 2), (2, 1): blocks(6, 2), (3, 0): blocks(4, 2), (3, 1): blocks(0, 2)}
+        k_sums = {(0, 0): blocks(2, 4), (0, 1): blocks(3, 4), (1, 0): blocks(5, 2), (1, 1): blocks(7, 2)}
+        products = {(0, 0): blocks(1, 2), (0, 1): blocks(1, 2), (1, 0): blocks(6, 2), (1, 1): blocks(3, 2)}
+        added = {}
+
+        def slot(i):
+            return ring[i][:].bitcast(F32)
+
+        def spent(s, c, block):
+            return chunks[s, c][:].rearrange("p e c -> p (e c)")[:, block * P :]
 
         def runs(pieces):
             found = []
-            for j, (d, vb) in enumerate(pieces):
-                if found and found[-1][1] + found[-1][2] == 2 * d + vb:
+            for j, (d, h) in enumerate(pieces):
+                if found and found[-1][1] + found[-1][2] == HALVES * d + h:
                     found[-1] = (found[-1][0], found[-1][1], found[-1][2] + 1)
                 else:
-                    found.append((j, 2 * d + vb, 1))
+                    found.append((j, HALVES * d + h, 1))
             return found
 
-        def copy(eng, dst, src):
-            if eng == "s":
-                nc.scalar.copy(dst, src)
-            else:
-                nc.vector.tensor_copy(dst, src)
+        def listed(first, count):
+            return offsets[:, LIST_COLS * first : LIST_COLS * (first + count)]
 
-        def gate_spread(ds):
-            spread = take("gate", [P, 2 * len(ds), P])
-            for i, d in enumerate(ds):
-                for vb in range(VB):
-                    nc.tensor.transpose(spread[:, 2 * i + vb, :], vec[:, vb, d : d + 1].to_broadcast([P, P]), ident[:])
-            nc.scalar.copy(gate_k[:, ds[0] * V : (ds[-1] + 1) * V], spread.rearrange("p j v -> p (j v)"))
-            give("gate")
+        def add_turned(bank_key, dst, src, total):
+            added[bank_key] = added.get(bank_key, 0) + 1
+            nc.tensor.matmul(
+                dst, lhsT=src, rhs=ident[:], start=(added[bank_key] == 1), stop=(added[bank_key] == total), is_transpose=True
+            )
 
-        def cast(s, c0, c1, eng):
-            if s not in pairs:
-                pairs[s] = keep.tile([P, 2 * T], BF16, name="pairs%d" % s)
-            base = max(c for c in BORDERS[s] if c <= c0)
-            dst = pairs[s][:, 2 * c0 : 2 * c1].rearrange("p (c e) -> p c e", e=2)
-            src = raw["pair", s, base][:, :, c0 - base : c1 - base].rearrange("p e c -> p c e")
-            if eng == "g":
-                nc.gpsimd.tensor_scalar(dst, src, 1.0, 0.0, ALU.mult, ALU.add)
-            else:
-                copy(eng, dst, src)
+        def spread_gates(first, count, bank):
+            spread = blocks(bank, HALVES * count)
+            for i in range(count):
+                for h in range(HALVES):
+                    repeated = gate_col[:, h, first + i : first + i + 1].to_broadcast([P, P])
+                    nc.tensor.transpose(spread[:, HALVES * i + h, :], repeated, ident[:])
+            nc.scalar.copy(gate_wide[:, first * V : (first + count) * V], spread.rearrange("p j v -> p (j v)"))
 
-        def front(s, pieces, engs):
+        def cast_views(s, c0, c1):
+            c = c0 // CHUNK
+            dst = pair_words[s][:, 2 * c0 : 2 * c1].rearrange("p (c e) -> p c e", e=2)
+            src = chunks[s, c][:, :, c0 - c * CHUNK : c1 - c * CHUNK].rearrange("p e c -> p c e")
+            return dst, src
+
+        def cast_on_scalar(s, c0, c1):
+            nc.scalar.copy(*cast_views(s, c0, c1))
+
+        def cast_on_gpsimd(s, c0, c1):
+            nc.gpsimd.tensor_scalar(*cast_views(s, c0, c1), 1.0, 0.0, ALU.mult, ALU.add)
+
+        def gather_words(s, pieces, buffer, bank):
             n = len(pieces)
-            picked = next_slot()
-            for j, first, run in runs(pieces):
-                nc.vector.tensor_copy(
-                    picked[:, j * P : (j + run) * P],
-                    pairs[s][:].bitcast(U32).indirect(offsets[:, 8 * first : 8 * (first + run)]),
-                )
-            turned = take("turned", [P, n, P])
+            picked = buffer.bitcast(U32)
+            for j, first, count in runs(pieces):
+                window = pair_words[s][:].bitcast(U32).indirect(listed(first, count))
+                nc.vector.tensor_copy(picked[:, j * P : (j + count) * P], window)
+            turned = blocks(bank, n)
             for j in range(n):
-                nc.tensor.transpose(turned[:, j, :], picked[:, j * P : (j + 1) * P].bitcast(F32), ident[:])
-            tile = fresh("scaled", [P, n, 2, P], F32)
-            for j, (d, vb) in enumerate(pieces):
+                nc.tensor.transpose(turned[:, j, :], buffer[:, j * P : (j + 1) * P], ident[:])
+            tile = keep.tile([P, n, 2, P], F32, name="scaled%d_%d%d" % (s, *pieces[0]))
+            for j, (d, h) in enumerate(pieces):
                 src = turned[:, j, :].bitcast(BF16).rearrange("v (p e) -> v e p", e=2)
-                weight = vec[:, vb, d : d + 1]
-                terms = 1
-                if engs[j] == "s":
-                    nc.scalar.activation(tile[:, j, :, :], src, ACT.Copy, scale=weight)
-                elif engs[j] == "v":
-                    nc.vector.tensor_scalar(tile[:, j, :, :], src, weight, None, ALU.mult)
-                else:
-                    key = [k for k in scaled if k[0] == s and k[2] == vb][-1]
-                    earlier, before = scaled.pop(key)
-                    terms += before
-                    nc.vector.scalar_tensor_tensor(tile[:, j, :, :], src, weight, earlier, ALU.mult, ALU.add)
-                scaled[s, d, vb] = (tile[:, j, :, :], terms)
-            give("turned")
+                nc.scalar.activation(tile[:, j, :, :], src, ACT.Copy, scale=gate_col[:, h, d : d + 1])
+                scaled[s, d, h] = tile[:, j, :, :]
 
-        def back(s, pieces):
-            a, u = divmod(s, 2)
-            for d, vb in pieces:
-                if (s, d, vb) not in scaled:
-                    continue
-                src, terms = scaled.pop((s, d, vb))
-                if (a, vb) not in acc:
-                    acc[a, vb] = take(("acc", a, vb), [P, 4, P])
-                    summed[a, vb] = 0
+        def sum_scaled(s, pieces):
+            for d, h in pieces:
                 for e in range(2):
-                    first = summed[a, vb] == 0
-                    summed[a, vb] += terms
-                    nc.tensor.matmul(
-                        acc[a, vb][:, 2 * u + e, :],
-                        lhsT=src[:, e, :],
-                        rhs=ident[:],
-                        start=first,
-                        stop=(summed[a, vb] == 4 * D),
-                        is_transpose=True,
-                    )
+                    add_turned(("k", h), k_sums[0, h][:, 2 * s + e, :], scaled[s, d, h][:, e, :], PACK * D)
 
-        def front_plain(s, e, pieces):
-            weighted = next_slot()[:].bitcast(F32)
-            for j, first, run in runs(pieces):
-                nc.vector.tensor_tensor(
-                    weighted[:, j * P : (j + run) * P],
-                    raw["plane", s, e][:].indirect(offsets[:, 8 * first : 8 * (first + run)]),
-                    gate_k[:, first * P : (first + run) * P],
-                    ALU.mult,
-                )
-            for j, (d, vb) in enumerate(pieces):
-                if (s, vb) not in mid:
-                    mid[s, vb] = take(("mid", s, vb), [P, 2, P])
-                    summed["mid", s, vb] = 0
-                summed["mid", s, vb] += 1
-                nc.tensor.matmul(
-                    mid[s, vb][:, e, :],
-                    lhsT=weighted[:, j * P : (j + 1) * P],
-                    rhs=ident[:],
-                    start=(summed["mid", s, vb] == 1),
-                    stop=(summed["mid", s, vb] == 2 * D),
-                    is_transpose=True,
-                )
+        def gather_plane(s, e, pieces, buffer):
+            for j, first, count in runs(pieces):
+                window = planes[s, e][:].indirect(listed(first, count))
+                weights = gate_wide[:, first * P : (first + count) * P]
+                nc.vector.tensor_tensor(buffer[:, j * P : (j + count) * P], window, weights, ALU.mult)
+            for j, (d, h) in enumerate(pieces):
+                add_turned(("bag", s, h), bag_sums[s, h][:, e, :], buffer[:, j * P : (j + 1) * P], 2 * D)
 
-        def mid_out(s, vb, eng):
-            words[s, vb] = fresh("words", [P, P, 2], BF16)
-            copy(eng, words[s, vb][:], mid[s, vb].rearrange("v e p -> v p e"))
-            give(("mid", s, vb))
+        def round_sums(s, h, buffer, copy):
+            rounded[s, h] = buffer[:, 0:P]
+            copy(rounded[s, h].bitcast(BF16).rearrange("v (p e) -> v p e", e=2), bag_sums[s, h].rearrange("v e p -> v p e"))
 
-        def back_words(s, vb):
-            a, u = divmod(s, 2)
-            if (a, vb) not in acc:
-                acc[a, vb] = take(("acc", a, vb), [P, 2, P])
-                as_words.add(a)
-            nc.tensor.transpose(acc[a, vb][:, u, :], words[s, vb][:].rearrange("v p e -> v (p e)").bitcast(F32), ident[:])
+        def turn_rounded(s, h):
+            nc.tensor.transpose(k_sums[1, h][:, s % 2, :], rounded[s, h], ident[:])
 
-        def sums_out(a, vb, eng):
-            dst = grouped[a][:, vb * P : (vb + 1) * P, :]
-            if a in as_words:
-                dst = dst.bitcast(F32)
-            copy(eng, dst, acc[a, vb].rearrange("p t v -> p v t"))
-            give(("acc", a, vb))
+        def interleave(a, h):
+            dst = grouped[a][:, h * P : (h + 1) * P, :]
+            nc.scalar.copy(dst if a == 0 else dst.bitcast(F32), k_sums[a, h].rearrange("p t v -> p v t"))
 
-        def quant(a, vbs):
-            n = len(vbs) * P
-            codes = keep.tile([P, n], U32, name="x_codes%d_%d" % (a, vbs[0]), align_bytes=64)
-            plane = keep.tile([P, n], U8, name="x_plane%d_%d" % (a, vbs[0]), align_bytes=64)
-            src = grouped[a][:, vbs[0] * P : vbs[0] * P + n, :]
+        def quantise(a, first, count):
+            codes = keep.tile([P, count * P], U32, name="x_codes%d_%d" % (a, first), align_bytes=64)
+            plane = keep.tile([P, count * P], U8, name="x_plane%d_%d" % (a, first), align_bytes=64)
+            src = grouped[a][:, first * P : (first + count) * P, :]
             nc.vector.quantize_mx(codes[:].bitcast(FP8X4), plane[:], src.rearrange("p v t -> p (v t)"))
-            for i, vb in enumerate(vbs):
-                x_codes[a, vb] = codes[:, i * P : (i + 1) * P]
-                x_plane[a, vb] = plane[:, i * P : (i + 1) * P]
+            for i in range(count):
+                x_codes[a, first + i] = codes[:, i * P : (i + 1) * P]
+                x_plane[a, first + i] = plane[:, i * P : (i + 1) * P]
 
-        def product(a, vb, m, bank):
-            if bank not in result:
-                result[bank] = take(("result", bank), [P, MB, P])
+        def multiply(a, h, m):
             cols = slice(m * P, (m + 1) * P)
             nc.tensor.matmul_mx(
-                result[bank][:, m, :],
+                products[h, m][:, m, :],
                 lhsT=w_codes[:, a, cols].bitcast(FP8X4),
                 lhsT_scale=w_plane[:, a, cols],
-                rhs=x_codes[a, vb].bitcast(FP8X4),
-                rhs_scale=x_plane[a, vb],
+                rhs=x_codes[a, h].bitcast(FP8X4),
+                rhs_scale=x_plane[a, h],
                 start=(a == 0),
                 stop=(a == PASSES - 1),
             )
 
-        def gelu(vb, m, bank):
-            nc.scalar.activation(final[vb][:, m, :], result[bank][:, m, :], ACT.Gelu_apprx_tanh, bias=bias[:, m : m + 1])
+        def gelu(h, m):
+            nc.scalar.activation(final[h][:, m, :], products[h, m][:, m, :], ACT.Gelu_apprx_tanh, bias=bias[:, m : m + 1])
 
-        def store(vb):
-            nc.sync.dma_start(out[:, vb * P : (vb + 1) * P].rearrange("(m p) v -> p m v", p=P), final[vb][:])
+        def store(h):
+            nc.sync.dma_start(out[:, h * P : (h + 1) * P].rearrange("(m p) v -> p m v", p=P), final[h][:])
 
-        steps = {"cast": cast, "front": front, "back": back, "out": sums_out, "quant": quant, "mm": product, "gelu": gelu, "store": store,
-                 "gateb": gate_spread, "frontm": front_plain, "midout": mid_out, "backw": back_words}
-        for step in PLAN:
-            steps[step[0]](*step[1:])
+        gather_plane(2, 0, LOW[:2], slot(0))
+        spread_gates(2, 2, 1)
+        cast_on_gpsimd(1, CHUNK, T)
+        cast_on_scalar(0, 0, SPLIT)
+        cast_on_scalar(0, CHUNK, T)
+        gather_plane(2, 1, LOW, slot(2))
+        gather_plane(2, 0, LOW[2:], slot(1))
+        gather_plane(2, 1, HIGH, slot(0))
+        cast_on_scalar(0, SPLIT, CHUNK)
+        gather_words(0, LOW, slot(1), 1)
+        gather_words(0, HIGH, slot(0), 5)
+        gather_plane(2, 0, HIGH, slot(2))
+        cast_on_gpsimd(1, 0, SPLIT)
+        sum_scaled(0, LOW)
+        cast_on_scalar(1, SPLIT, CHUNK)
+        gather_words(1, LOW, slot(2), 1)
+        gather_words(1, HIGH[:3], slot(1), 5)
+        round_sums(2, 1, spent(0, 1, 4), nc.scalar.copy)
+        sum_scaled(0, HIGH)
+        sum_scaled(1, LOW)
+        round_sums(2, 0, spent(0, 1, 2), nc.scalar.copy)
+        gather_words(1, HIGH[3:], spent(1, 0, 4), 1)
+        gather_plane(3, 0, LOW, spent(1, 1, 0))
+        sum_scaled(1, HIGH)
+        gather_plane(3, 1, LOW[0::2], spent(0, 0, 2))
+        gather_plane(3, 0, HIGH, slot(2))
+        gather_plane(3, 1, HIGH[0::2], slot(0))
+        gather_plane(3, 1, LOW[1::2], spent(1, 1, 6))
+        interleave(0, 1)
+        turn_rounded(2, 0)
+        interleave(0, 0)
+        gather_plane(3, 1, HIGH[1::2], slot(1))
+        quantise(0, 0, HALVES)
+        round_sums(3, 0, spent(0, 1, 0), nc.scalar.copy)
+        turn_rounded(3, 0)
+        multiply(0, 1, 0)
+        turn_rounded(2, 1)
+        last_rounded = keep.tile([P, P], F32, name="last_rounded")
+        round_sums(3, 1, last_rounded[:], nc.vector.tensor_copy)
+        multiply(0, 0, 0)
+        interleave(1, 0)
+        quantise(1, 0, 1)
+        turn_rounded(3, 1)
+        interleave(1, 1)
+        multiply(1, 0, 0)
+        multiply(0, 0, 1)
+        quantise(1, 1, 1)
+        multiply(1, 0, 1)
+        gelu(0, 1)
+        gelu(0, 0)
+        store(0)
+        multiply(0, 1, 1)
+        multiply(1, 1, 1)
+        gelu(1, 1)
+        multiply(1, 1, 0)
+        gelu(1, 0)
+        store(1)

from contextlib import ExitStack

import concourse.mybir as mybir

K, T, D, V, N = 1024, 1024, 4, 256, 256
FLOPS = 2 * K * N * V

F32 = mybir.dt.float32
BF16 = mybir.dt.bfloat16
U32 = mybir.dt.uint32
I32 = mybir.dt.int32
U16 = mybir.dt.uint16
U8 = mybir.dt.uint8
FP8X4 = mybir.dt.float8_e4m3fn_x4
ACT = mybir.ActivationFunctionType
ALU = mybir.AluOpType

P = 128
PACK = 4
K_PASS = P * PACK
PASSES = K // K_PASS
HALVES = V // P
M_BLOCKS = N // P
QUAD = 32
BANK = 512
CHUNK = T // 2
SPLIT = 128
LIST_COLS = P // 16
GATE_COLS = 8

LOW = ((0, 0), (0, 1), (1, 0), (1, 1))
HIGH = ((2, 0), (2, 1), (3, 0), (3, 1))


def tile_picked_bag_lin_gelu_sub_l_kernel(tc, xT, w_words, w_scales, b, gate, offs, out):
    nc = tc.nc
    with ExitStack() as ctx:
        keep = ctx.enter_context(tc.tile_pool(name="keep", bufs=1))
        psum = ctx.enter_context(tc.psum_pool(name="psum", bufs=1))
        banks = [psum.tile([P, BANK], F32, name="bank%d" % i) for i in range(8)]
        ring = [keep.tile([P, 4 * P], U32, name="ring%d" % i) for i in range(3)]

        def blocks(bank, n):
            return banks[bank][:, 0 : n * P].rearrange("p (j c) -> p j c", c=P)

        offsets = keep.tile([P, D * V // 16], U16, name="offsets")
        gate_rows = keep.tile([P, V], F32, name="gate_rows")
        nc.vector.memset(gate_rows[:], 0.0)
        nc.sync.dma_start(gate_rows[0:D, :], gate[:, 0, :])
        gate_wide = keep.tile([P, D * V], F32, name="gate_wide")
        planes = {}
        chunks = {}

        def pass_rows(a):
            return xT[K_PASS * a : K_PASS * (a + 1), :].rearrange("(p t) c -> p t c", t=PACK)

        def load_plane(s, e):
            planes[s, e] = keep.tile([P, T], F32, name="plane%d_%d" % (s, e))
            nc.sync.dma_start(planes[s, e][:], pass_rows(s // 2)[:, 2 * (s % 2) + e, :])

        load_plane(2, 0)
        nc.sync.dma_start(gate_wide[:, 0:V], gate[0])
        nc.sync.dma_start(offsets[:], offs)
        nc.sync.dma_start(gate_wide[:, V : 2 * V], gate[1])
        load_plane(2, 1)
        for s in range(2):
            for c in range(T // CHUNK):
                chunks[s, c] = keep.tile([P, 2, CHUNK], F32, name="chunk%d_%d" % (s, c))
                nc.sync.dma_start(chunks[s, c][:], pass_rows(0)[:, 2 * s : 2 * s + 2, c * CHUNK : (c + 1) * CHUNK])
        load_plane(3, 0)
        load_plane(3, 1)

        ident = keep.tile([P, P], F32, name="ident")
        ones = keep.tile([P, P], F32, name="ones")
        column = keep.tile([P, P], F32, name="column", align_bytes=64)
        in_quadrant = keep.tile([P, QUAD], F32, name="in_quadrant", align_bytes=64)
        quadrant = keep.tile([P, 1], F32, name="quadrant")
        nc.vector.memset(ones[:], 1.0)
        for q in range(P // QUAD):
            nc.vector.memset(quadrant[QUAD * q : QUAD * (q + 1), :], float(QUAD * q))
        nc.vector.tensor_tensor_scan(column[:], ones[:], ones[:], -1.0, ALU.mult, ALU.add)
        nc.vector.transpose(in_quadrant[:], column[:, 0:QUAD])
        nc.vector.tensor_scalar(ident[:], column[:], in_quadrant[:, 0:1], quadrant[:], ALU.subtract, ALU.is_equal)

        warm_in = keep.tile([P, 8], F32, name="warm_in")
        nc.vector.memset(warm_in[:], 0.0)
        warm_out = keep.tile([P, 8], F32, name="warm_out")
        nc.scalar.activation(warm_out[:], warm_in[:], ACT.Gelu_apprx_tanh)

        for h in range(HALVES):
            nc.tensor.transpose(blocks(0, HALVES)[:, h, :], gate_rows[:, h * P : (h + 1) * P], ident[:])
        gate_col = keep.tile([P, HALVES, GATE_COLS], F32, name="gate_col")
        nc.scalar.copy(gate_col[:], blocks(0, HALVES)[:, :, 0:GATE_COLS])

        w_codes = keep.tile([P, PASSES, N], U32, name="w_codes", align_bytes=64)
        w_plane = keep.tile([P, PASSES, N], U8, name="w_plane", align_bytes=64)
        nc.vector.memset(w_plane[:].rearrange("p a m -> p (a m)").bitcast(I32), 0)
        nc.sync.dma_start(w_codes[:].bitcast(I32), w_words.rearrange("a p m r -> p a (m r)").bitcast(I32))
        bias = keep.tile([P, M_BLOCKS], F32, name="bias")
        with nc.allow_non_contiguous_dma(reason="one bias value a partition"):
            nc.sync.dma_start(bias[:], b.rearrange("(m p) o -> p (m o)", p=P))
        for q in range(P // QUAD):
            nc.sync.dma_start(
                w_plane[QUAD * q : QUAD * q + 4, :, :].bitcast(I32),
                w_scales[:, 4 * q : 4 * q + 4, :].rearrange("a r m -> r a m").bitcast(I32),
            )

        grouped = [keep.tile([P, V, PACK], BF16, name="grouped%d" % a, align_bytes=64) for a in range(PASSES)]
        final = [keep.tile([P, M_BLOCKS, P], F32, name="final%d" % h) for h in range(HALVES)]
        pair_words = [keep.tile([P, 2 * T], BF16, name="pair_words%d" % s) for s in range(2)]
        scaled = {}
        rounded = {}
        x_codes = {}
        x_plane = {}

        bag_sums = {(2, 0): blocks(7, 2), (2, 1): blocks(6, 2), (3, 0): blocks(4, 2), (3, 1): blocks(0, 2)}
        k_sums = {(0, 0): blocks(2, 4), (0, 1): blocks(3, 4), (1, 0): blocks(5, 2), (1, 1): blocks(7, 2)}
        products = {(0, 0): blocks(1, 2), (0, 1): blocks(1, 2), (1, 0): blocks(6, 2), (1, 1): blocks(3, 2)}
        added = {}

        def slot(i):
            return ring[i][:].bitcast(F32)

        def spent(s, c, block):
            return chunks[s, c][:].rearrange("p e c -> p (e c)")[:, block * P :]

        def runs(pieces):
            found = []
            for j, (d, h) in enumerate(pieces):
                if found and found[-1][1] + found[-1][2] == HALVES * d + h:
                    found[-1] = (found[-1][0], found[-1][1], found[-1][2] + 1)
                else:
                    found.append((j, HALVES * d + h, 1))
            return found

        def listed(first, count):
            return offsets[:, LIST_COLS * first : LIST_COLS * (first + count)]

        def add_turned(bank_key, dst, src, total):
            added[bank_key] = added.get(bank_key, 0) + 1
            nc.tensor.matmul(
                dst, lhsT=src, rhs=ident[:], start=(added[bank_key] == 1), stop=(added[bank_key] == total), is_transpose=True
            )

        def spread_gates(first, count, bank):
            spread = blocks(bank, HALVES * count)
            for i in range(count):
                for h in range(HALVES):
                    repeated = gate_col[:, h, first + i : first + i + 1].to_broadcast([P, P])
                    nc.tensor.transpose(spread[:, HALVES * i + h, :], repeated, ident[:])
            nc.scalar.copy(gate_wide[:, first * V : (first + count) * V], spread.rearrange("p j v -> p (j v)"))

        def cast_views(s, c0, c1):
            c = c0 // CHUNK
            dst = pair_words[s][:, 2 * c0 : 2 * c1].rearrange("p (c e) -> p c e", e=2)
            src = chunks[s, c][:, :, c0 - c * CHUNK : c1 - c * CHUNK].rearrange("p e c -> p c e")
            return dst, src

        def cast_on_scalar(s, c0, c1):
            nc.scalar.copy(*cast_views(s, c0, c1))

        def cast_on_gpsimd(s, c0, c1):
            nc.gpsimd.tensor_scalar(*cast_views(s, c0, c1), 1.0, 0.0, ALU.mult, ALU.add)

        def gather_words(s, pieces, buffer, bank):
            n = len(pieces)
            picked = buffer.bitcast(U32)
            for j, first, count in runs(pieces):
                window = pair_words[s][:].bitcast(U32).indirect(listed(first, count))
                nc.vector.tensor_copy(picked[:, j * P : (j + count) * P], window)
            turned = blocks(bank, n)
            for j in range(n):
                nc.tensor.transpose(turned[:, j, :], buffer[:, j * P : (j + 1) * P], ident[:])
            tile = keep.tile([P, n, 2, P], F32, name="scaled%d_%d%d" % (s, *pieces[0]))
            for j, (d, h) in enumerate(pieces):
                src = turned[:, j, :].bitcast(BF16).rearrange("v (p e) -> v e p", e=2)
                nc.scalar.activation(tile[:, j, :, :], src, ACT.Copy, scale=gate_col[:, h, d : d + 1])
                scaled[s, d, h] = tile[:, j, :, :]

        def sum_scaled(s, pieces):
            for d, h in pieces:
                for e in range(2):
                    add_turned(("k", h), k_sums[0, h][:, 2 * s + e, :], scaled[s, d, h][:, e, :], PACK * D)

        def gather_plane(s, e, pieces, buffer):
            for j, first, count in runs(pieces):
                window = planes[s, e][:].indirect(listed(first, count))
                weights = gate_wide[:, first * P : (first + count) * P]
                nc.vector.tensor_tensor(buffer[:, j * P : (j + count) * P], window, weights, ALU.mult)
            for j, (d, h) in enumerate(pieces):
                add_turned(("bag", s, h), bag_sums[s, h][:, e, :], buffer[:, j * P : (j + 1) * P], 2 * D)

        def round_sums(s, h, buffer, copy):
            rounded[s, h] = buffer[:, 0:P]
            copy(rounded[s, h].bitcast(BF16).rearrange("v (p e) -> v p e", e=2), bag_sums[s, h].rearrange("v e p -> v p e"))

        def turn_rounded(s, h):
            nc.tensor.transpose(k_sums[1, h][:, s % 2, :], rounded[s, h], ident[:])

        def interleave(a, h):
            dst = grouped[a][:, h * P : (h + 1) * P, :]
            nc.scalar.copy(dst if a == 0 else dst.bitcast(F32), k_sums[a, h].rearrange("p t v -> p v t"))

        def quantise(a, first, count):
            codes = keep.tile([P, count * P], U32, name="x_codes%d_%d" % (a, first), align_bytes=64)
            plane = keep.tile([P, count * P], U8, name="x_plane%d_%d" % (a, first), align_bytes=64)
            src = grouped[a][:, first * P : (first + count) * P, :]
            nc.vector.quantize_mx(codes[:].bitcast(FP8X4), plane[:], src.rearrange("p v t -> p (v t)"))
            for i in range(count):
                x_codes[a, first + i] = codes[:, i * P : (i + 1) * P]
                x_plane[a, first + i] = plane[:, i * P : (i + 1) * P]

        def multiply(a, h, m):
            cols = slice(m * P, (m + 1) * P)
            nc.tensor.matmul_mx(
                products[h, m][:, m, :],
                lhsT=w_codes[:, a, cols].bitcast(FP8X4),
                lhsT_scale=w_plane[:, a, cols],
                rhs=x_codes[a, h].bitcast(FP8X4),
                rhs_scale=x_plane[a, h],
                start=(a == 0),
                stop=(a == PASSES - 1),
            )

        def gelu(h, m):
            nc.scalar.activation(final[h][:, m, :], products[h, m][:, m, :], ACT.Gelu_apprx_tanh, bias=bias[:, m : m + 1])

        def store(h):
            nc.sync.dma_start(out[:, h * P : (h + 1) * P].rearrange("(m p) v -> p m v", p=P), final[h][:])

        gather_plane(2, 0, LOW[:2], slot(0))
        spread_gates(2, 2, 1)
        cast_on_gpsimd(1, CHUNK, T)
        cast_on_scalar(0, 0, SPLIT)
        cast_on_scalar(0, CHUNK, T)
        gather_plane(2, 1, LOW, slot(2))
        gather_plane(2, 0, LOW[2:], slot(1))
        gather_plane(2, 1, HIGH, slot(0))
        cast_on_scalar(0, SPLIT, CHUNK)
        gather_words(0, LOW, slot(1), 1)
        gather_words(0, HIGH, slot(0), 5)
        gather_plane(2, 0, HIGH, slot(2))
        cast_on_gpsimd(1, 0, SPLIT)
        sum_scaled(0, LOW)
        cast_on_scalar(1, SPLIT, CHUNK)
        gather_words(1, LOW, slot(2), 1)
        gather_words(1, HIGH[:3], slot(1), 5)
        round_sums(2, 1, spent(0, 1, 4), nc.scalar.copy)
        sum_scaled(0, HIGH)
        sum_scaled(1, LOW)
        round_sums(2, 0, spent(0, 1, 2), nc.scalar.copy)
        gather_words(1, HIGH[3:], spent(1, 0, 4), 1)
        gather_plane(3, 0, LOW, spent(1, 1, 0))
        sum_scaled(1, HIGH)
        gather_plane(3, 1, LOW[0::2], spent(0, 0, 2))
        gather_plane(3, 0, HIGH, slot(2))
        gather_plane(3, 1, HIGH[0::2], slot(0))
        gather_plane(3, 1, LOW[1::2], spent(1, 1, 6))
        interleave(0, 1)
        turn_rounded(2, 0)
        interleave(0, 0)
        gather_plane(3, 1, HIGH[1::2], slot(1))
        quantise(0, 0, HALVES)
        round_sums(3, 0, spent(0, 1, 0), nc.scalar.copy)
        turn_rounded(3, 0)
        multiply(0, 1, 0)
        turn_rounded(2, 1)
        last_rounded = keep.tile([P, P], F32, name="last_rounded")
        round_sums(3, 1, last_rounded[:], nc.vector.tensor_copy)
        multiply(0, 0, 0)
        interleave(1, 0)
        quantise(1, 0, 1)
        turn_rounded(3, 1)
        interleave(1, 1)
        multiply(1, 0, 0)
        multiply(0, 0, 1)
        quantise(1, 1, 1)
        multiply(1, 0, 1)
        gelu(0, 1)
        gelu(0, 0)
        store(0)
        multiply(0, 1, 1)
        multiply(1, 1, 1)
        gelu(1, 1)
        multiply(1, 1, 0)
        gelu(1, 0)
        store(1)
